import numpy as np
import ml_dtypes


def mxq(x, axis, fmt="e4m3"):
    dtype, down = {"e4m3": (ml_dtypes.float8_e4m3fn, 7), "e5m2": (ml_dtypes.float8_e5m2, 14)}[fmt]
    v = np.moveaxis(np.asarray(x, np.float32).astype(ml_dtypes.bfloat16).astype(np.float64), axis, -1)
    blocks = v.reshape(v.shape[:-1] + (-1, 32))
    amax = np.abs(blocks).max(-1, keepdims=True)
    byte = np.maximum(np.where(amax > 0, np.frexp(amax)[1] - 1 + 127, 0) - down, 1)
    scale = np.exp2(byte - 127.0)
    codes = (blocks / scale).astype(np.float32).astype(dtype).astype(np.float64)
    return np.moveaxis((codes * scale).reshape(v.shape), -1, axis)


WIDE = False


def mx_kscale(k):
    if not WIDE:
        return np.ones(k)
    levels = np.array([10, -10, 5, -5, 0])
    if k % 512:
        return np.exp2(np.random.permutation(np.resize(levels, k // 32))).repeat(32)
    a = np.empty((k // 512, 16))
    for p in range(k // 512):
        a[p, :8] = np.random.permutation(np.resize(levels, 8))
        for g in range(8):
            far = levels[np.abs(levels - a[p, g]) >= 10]
            a[p, g + 8] = far[np.random.randint(len(far))]
    return np.exp2(a.ravel()).repeat(32)


def f64(x):
    return np.asarray(x).astype(np.float64)


def striped(idx):
    return np.tile(idx.reshape(-1, 16).T, (8, 1)).astype(np.uint16)


def unstriped(offs):
    return offs[:16].T.reshape(-1).astype(np.int64)


E2M1 = np.array([0.0, 0.5, 1.0, 1.5, 2.0, 3.0, 4.0, 6.0, -0.0, -0.5, -1.0, -1.5, -2.0, -3.0, -4.0, -6.0])


def pack_fp4(w):
    k, n = w.shape
    w = f64(np.asarray(w, np.float32).astype(ml_dtypes.bfloat16)).reshape(k // 32, 32, n)
    amax = np.abs(w).max(1)
    mant, ex = np.frexp(amax / 6.0)
    byte = np.clip(np.where(amax > 0, np.where(mant > 0.5, ex, ex - 1) + 127, 1), 1, 254)
    scaled = (w * np.exp2(127.0 - byte)[:, None, :]).reshape(k, n).astype(np.float32)
    c = np.ascontiguousarray(scaled.reshape(k // 512, 128, 4, n).transpose(0, 1, 3, 2)).astype(ml_dtypes.float4_e2m1fn).view(np.uint8) & 0xF
    words = (c[..., 0::2] | (c[..., 1::2] << 4)).reshape(k // 512, 128, 2 * n)
    return np.ascontiguousarray(words), np.ascontiguousarray(byte.astype(np.uint8).reshape(k // 512, 16, n))


def unpack_fp4(words, scales):
    g, _, n = scales.shape
    words = np.ascontiguousarray(words).reshape(g, 128, n, 2)
    nib = np.empty((g, 128, n, 4), np.uint8)
    nib[..., 0::2] = words & 0xF
    nib[..., 1::2] = words >> 4
    vals = E2M1[nib] * np.repeat(np.exp2(scales.astype(np.float64) - 127.0), 8, axis=1)[..., None]
    return vals.transpose(0, 1, 3, 2).reshape(g * 512, n)


K, T, S, N = 512, 1024, 512, 128
P = 2 ** 7


def setup_inputs():
    n = np.random.standard_normal
    s = mx_kscale(K)[:, None]
    packed_w1 = pack_fp4(n((K, N)) / np.sqrt(K) / s)
    return {
        "xT": (n((K, T)) * s).astype(np.float32),
        "mean": np.tile(0.3 * np.random.standard_normal(T), (P, 1)).astype(np.float32),
        "inv": np.tile(np.random.uniform(0.5, 2.0, T), (P, 1)).astype(np.float32),
        "gsum": n((N, 1)).astype(np.float32),
        "b": (0.3 * n((N, 1))).astype(np.float32),
        "w1_words": packed_w1[0],
        "w1_scales": packed_w1[1],
        "offs": striped(np.random.permutation(T)[:S]),
    }


def reference(xT, mean, inv, gsum, b, w1_words, w1_scales, offs):
    xq = mxq(f64(xT)[:, unstriped(offs)], 0, "e4m3")
    y = unpack_fp4(w1_words, w1_scales).T @ xq
    mg = f64(mean)[:1][:, unstriped(offs)]
    ig = f64(inv)[:1][:, unstriped(offs)]
    return (y - (f64(gsum) * mg)) * ig + f64(b)

@@ -1,0 +1,144 @@
+from contextlib import ExitStack
+
+import concourse.mybir as mybir
+from concourse.masks import make_identity
+
+K, T, S, N = 512, 1024, 512, 128
+FLOPS = 2 * K * N * S
+BYTES = K * T * 4 + 2 * T * 4 + 2 * N * 4 + 128 * 256 + 16 * 128 + 128 * 32 * 2 + N * S * 4
+
+F32 = mybir.dt.float32
+BF16 = mybir.dt.bfloat16
+U32 = mybir.dt.uint32
+I32 = mybir.dt.int32
+U16 = mybir.dt.uint16
+U8 = mybir.dt.uint8
+FP8X4 = mybir.dt.float8_e4m3fn_x4
+FP4X4 = mybir.dt.float4_e2m1fn_x4
+MULT = mybir.AluOpType.mult
+ADD = mybir.AluOpType.add
+SUB = mybir.AluOpType.subtract
+IDENT = mybir.ActivationFunctionType.Identity
+COPY = mybir.ActivationFunctionType.Copy
+
+P = 128
+CH = 128
+NCH = S // CH
+MEAN_ROW, INV_ROW = P - 2, P - 1
+LOADS = [(0, 0, 512, [("s", 0, 512)]), (0, 512, 1024, [("v", 512, 864), ("s", 864, 1024)]), (1, 0, 512, [("s", 0, 512)]), (1, 512, 896, [("v", 512, 896)]), (1, 896, 1024, [("v", 896, 1024)])]
+STEPPED = ()
+
+
+def tile_picked_lnfold_none_l_kernel(tc, xT, mean, inv, gsum, b, w1_words, w1_scales, offs, out):
+    nc = tc.nc
+    with ExitStack() as ctx:
+        keep = ctx.enter_context(tc.tile_pool(name="keep", bufs=1))
+        psum = ctx.enter_context(tc.psum_pool(name="psum", bufs=1))
+
+        offsets = keep.tile([P, S // 16], U16, name="offsets")
+        nc.sync.dma_start(offsets[:], offs)
+
+        stats = keep.tile([P, T], F32, name="stats", tag="pair0")
+        g_col = keep.tile([P, 1], F32, name="g_col")
+        nc.scalar.dma_start(stats[MEAN_ROW : MEAN_ROW + 1, :], mean[0:1, :])
+        nc.scalar.dma_start(stats[INV_ROW : INV_ROW + 1, :], inv[0:1, :])
+        nc.scalar.dma_start(g_col[:], gsum)
+        zero = keep.tile([P, 1], F32, name="zero", tag="pair1")
+        warm = keep.tile([P, 1], F32, name="warm")
+        nc.vector.memset(zero[:], 0.0)
+        nc.scalar.activation(warm[:], zero[:], IDENT, bias=zero[:])
+        nc.vector.memset(stats[0:MEAN_ROW, :], 0.0)
+
+        x_rows = xT.rearrange("(p j) w -> p j w", j=4)
+        raws = []
+        for i, (u, c0, c1, shares) in enumerate(LOADS):
+            raw = keep.tile([P, 2, c1 - c0], F32, name="raw%d" % i)
+            nc.sync.dma_start(raw[:], x_rows[:, 2 * u : 2 * u + 2, c0:c1])
+            raws.append(raw)
+
+        b_col = keep.tile([P, 1], F32, name="b_col")
+        w_words = keep.tile([P, 2 * N], U8, name="w_words", align_bytes=64)
+        w_scales = keep.tile([P, N], U8, name="w_scales", align_bytes=64)
+        nc.sync.dma_start(w_words[:].bitcast(I32), w1_words[0].bitcast(I32))
+
+        ident = keep.tile([P, P], F32, name="ident")
+        make_identity(nc, ident[:])
+        nc.gpsimd.memset(w_scales[:].bitcast(I32), 0)
+        for q in range(4):
+            nc.sync.dma_start(w_scales[32 * q : 32 * q + 4, :].bitcast(I32), w1_scales[0, 4 * q : 4 * q + 4, :].bitcast(I32))
+        nc.sync.dma_start(b_col[:], b)
+
+        picked = [keep.tile([P, S // 2], F32, name="picked%d" % h) for h in range(2)]
+        turned = psum.tile([P, NCH, P], F32, name="turned")
+        for h in range(2):
+            nc.vector.tensor_copy(picked[h][:], stats[:].indirect(offsets[:, 16 * h : 16 * (h + 1)]))
+            for c in range(2):
+                nc.tensor.transpose(turned[:, 2 * h + c, :], picked[h][:, c * CH : (c + 1) * CH], ident[:])
+        g_ps = psum.tile([P, N], F32, name="g_ps")
+        nc.tensor.transpose(g_ps[:], g_col[:].to_broadcast([P, P]), ident[:])
+        inv_c = keep.tile([P, NCH], F32, name="inv_c")
+        mean_c = keep.tile([P, NCH], F32, name="mean_c", tag="halves2")
+        nc.scalar.copy(inv_c[:], turned[:, :, INV_ROW])
+        nc.scalar.activation(mean_c[:], turned[:, :, MEAN_ROW], IDENT, bias=zero[:])
+        inv_ps = psum.tile([P, S], F32, name="inv_ps")
+        for c in range(NCH):
+            nc.tensor.transpose(inv_ps[:, c * CH : (c + 1) * CH], inv_c[:, c : c + 1].to_broadcast([P, P]), ident[:])
+        mi = keep.tile([P, NCH], F32, name="mi", tag="woven0", align_bytes=64)
+        nc.vector.tensor_tensor(mi[:], mean_c[:], inv_c[:], MULT)
+
+        pairs = [keep.tile([P, 2 * T], BF16, name="pair%d" % u, tag="pair%d" % u) for u in range(2)]
+
+        def cast(i):
+            u, c0, c1, shares = LOADS[i]
+            for eng, a, z in shares:
+                dst = pairs[u][:, 2 * a : 2 * z].rearrange("p (c j) -> p c j", j=2)
+                src = raws[i][:, :, a - c0 : z - c0].rearrange("p j c -> p c j")
+                if eng == "v":
+                    nc.vector.tensor_copy(dst, src)
+                else:
+                    nc.scalar.copy(dst, src)
+
+        halves = [keep.tile([P, 2, CH], U32, name="halves%d" % c, tag="halves%d" % c) for c in range(NCH)]
+        woven = [keep.tile([P, CH, 2], U32, name="woven%d" % c, tag="woven%d" % c, align_bytes=64) for c in range(NCH)]
+
+        def gather(u, c):
+            dst = woven[c][:, :, u] if c in STEPPED else halves[c][:, u, :]
+            nc.vector.tensor_copy(dst, pairs[u][:].bitcast(U32).indirect(offsets[:, c * (CH // 16) : (c + 1) * (CH // 16)]))
+
+        inv_bc = keep.tile([P, S], F32, name="inv_bc")
+
+        for i in range(len(LOADS)):
+            if LOADS[i][0] == 0:
+                cast(i)
+        for c in range(NCH):
+            gather(0, c)
+        for i in range(len(LOADS)):
+            if LOADS[i][0] == 1:
+                cast(i)
+        gm_ps = psum.tile([P, S], F32, name="gm_ps")
+        gm_t = [keep.tile([P, N], F32, name="gm_t%d" % c) for c in range(NCH)]
+        for c in range(NCH):
+            nc.scalar.activation(gm_t[c][:], g_ps[:], COPY, scale=mi[:, c : c + 1])
+            nc.tensor.transpose(gm_ps[:, c * CH : (c + 1) * CH], gm_t[c][:], ident[:])
+        nc.scalar.copy(inv_bc[:], inv_ps[:])
+
+        codes = [keep.tile([P, CH], U32, name="codes%d" % c, align_bytes=64) for c in range(NCH)]
+        planes = [keep.tile([P, CH], U8, name="plane%d" % c, align_bytes=64) for c in range(NCH)]
+        accs = [psum.tile([P, CH], F32, name="acc%d" % c) for c in range(NCH)]
+        scaled = [keep.tile([P, CH], F32, name="scaled%d" % c) for c in range(NCH)]
+        result = [keep.tile([P, CH], F32, name="result%d" % c) for c in range(NCH)]
+
+        for c in range(NCH):
+            gather(1, c)
+            if c not in STEPPED:
+                nc.scalar.copy(woven[c][:], halves[c][:].rearrange("p u s -> p s u"))
+        for c in range(NCH):
+            nc.vector.quantize_mx(out=codes[c][:].bitcast(FP8X4), scales=planes[c][:], in_=woven[c][:].rearrange("p s u -> p (s u)").bitcast(BF16))
+            nc.tensor.matmul_mx(accs[c][:], lhsT=w_words[:].bitcast(FP4X4), lhsT_scale=w_scales[:], rhs=codes[c][:].bitcast(FP8X4), rhs_scale=planes[c][:], start=True, stop=True)
+        for kind, c in [("m", 0), ("m", 1), ("a", 0), ("m", 2), ("a", 1), ("m", 3), ("a", 2), ("a", 3)]:
+            cs = slice(c * CH, (c + 1) * CH)
+            if kind == "m":
+                nc.vector.tensor_tensor(scaled[c][:], accs[c][:], inv_bc[:, cs], MULT)
+            else:
+                nc.vector.scalar_tensor_tensor(result[c][:], scaled[c][:], b_col[:], gm_ps[:, cs], ADD, SUB)
+                nc.sync.dma_start(out[:, cs], result[c][:])

@@ -25,7 +25,7 @@ P = 128
 CH = 128
 NCH = S // CH
 MEAN_ROW, INV_ROW = P - 2, P - 1
-LOADS = [(0, 0, 512, [("s", 0, 512)]), (0, 512, 1024, [("v", 512, 864), ("s", 864, 1024)]), (1, 0, 512, [("s", 0, 512)]), (1, 512, 896, [("v", 512, 896)]), (1, 896, 1024, [("v", 896, 1024)])]
+LOADS = [(0, 0, 512, [("s", 0, 512)]), (0, 512, 1024, [("v", 512, 896), ("s", 896, 1024)]), (1, 0, 512, [("s", 0, 512)]), (1, 512, 896, [("v", 512, 896)]), (1, 896, 1024, [("v", 896, 1024)])]
 STEPPED = ()
 
 
@@ -38,10 +38,10 @@ def tile_picked_lnfold_none_l_kernel(tc, xT, mean, inv, gsum, b, w1_words, w1_sc
         offsets = keep.tile([P, S // 16], U16, name="offsets")
         nc.sync.dma_start(offsets[:], offs)
 
-        stats = keep.tile([P, T], F32, name="stats", tag="pair0")
+        stats = keep.tile([P, T], F32, name="stats")
         g_col = keep.tile([P, 1], F32, name="g_col")
         nc.scalar.dma_start(stats[MEAN_ROW : MEAN_ROW + 1, :], mean[0:1, :])
-        nc.scalar.dma_start(stats[INV_ROW : INV_ROW + 1, :], inv[0:1, :])
+        nc.sync.dma_start(stats[INV_ROW : INV_ROW + 1, :], inv[0:1, :])
         nc.scalar.dma_start(g_col[:], gsum)
         zero = keep.tile([P, 1], F32, name="zero", tag="pair1")
         warm = keep.tile([P, 1], F32, name="warm")
@@ -77,7 +77,7 @@ def tile_picked_lnfold_none_l_kernel(tc, xT, mean, inv, gsum, b, w1_words, w1_sc
         g_ps = psum.tile([P, N], F32, name="g_ps")
         nc.tensor.transpose(g_ps[:], g_col[:].to_broadcast([P, P]), ident[:])
         inv_c = keep.tile([P, NCH], F32, name="inv_c")
-        mean_c = keep.tile([P, NCH], F32, name="mean_c", tag="halves2")
+        mean_c = keep.tile([P, NCH], F32, name="mean_c", tag="halves1")
         nc.scalar.copy(inv_c[:], turned[:, :, INV_ROW])
         nc.scalar.activation(mean_c[:], turned[:, :, MEAN_ROW], IDENT, bias=zero[:])
         inv_ps = psum.tile([P, S], F32, name="inv_ps")

@@ -40,7 +40,7 @@ def tile_picked_lnfold_none_l_kernel(tc, xT, mean, inv, gsum, b, w1_words, w1_sc
 
         stats = keep.tile([P, T], F32, name="stats")
         g_col = keep.tile([P, 1], F32, name="g_col")
-        nc.scalar.dma_start(stats[MEAN_ROW : MEAN_ROW + 1, :], mean[0:1, :])
+        nc.sync.dma_start(stats[MEAN_ROW : MEAN_ROW + 1, :], mean[0:1, :])
         nc.sync.dma_start(stats[INV_ROW : INV_ROW + 1, :], inv[0:1, :])
         nc.scalar.dma_start(g_col[:], gsum)
         zero = keep.tile([P, 1], F32, name="zero", tag="pair1")
@@ -52,7 +52,7 @@ def tile_picked_lnfold_none_l_kernel(tc, xT, mean, inv, gsum, b, w1_words, w1_sc
         x_rows = xT.rearrange("(p j) w -> p j w", j=4)
         raws = []
         for i, (u, c0, c1, shares) in enumerate(LOADS):
-            raw = keep.tile([P, 2, c1 - c0], F32, name="raw%d" % i)
+            raw = keep.tile([P, 2, c1 - c0], F32, name="raw%d" % i, tag="raw%d" % i)
             nc.sync.dma_start(raw[:], x_rows[:, 2 * u : 2 * u + 2, c0:c1])
             raws.append(raw)
 
@@ -77,14 +77,13 @@ def tile_picked_lnfold_none_l_kernel(tc, xT, mean, inv, gsum, b, w1_words, w1_sc
         g_ps = psum.tile([P, N], F32, name="g_ps")
         nc.tensor.transpose(g_ps[:], g_col[:].to_broadcast([P, P]), ident[:])
         inv_c = keep.tile([P, NCH], F32, name="inv_c")
-        mean_c = keep.tile([P, NCH], F32, name="mean_c", tag="halves1")
         nc.scalar.copy(inv_c[:], turned[:, :, INV_ROW])
-        nc.scalar.activation(mean_c[:], turned[:, :, MEAN_ROW], IDENT, bias=zero[:])
         inv_ps = psum.tile([P, S], F32, name="inv_ps")
         for c in range(NCH):
             nc.tensor.transpose(inv_ps[:, c * CH : (c + 1) * CH], inv_c[:, c : c + 1].to_broadcast([P, P]), ident[:])
-        mi = keep.tile([P, NCH], F32, name="mi", tag="woven0", align_bytes=64)
-        nc.vector.tensor_tensor(mi[:], mean_c[:], inv_c[:], MULT)
+        mi = keep.tile([P, NCH], F32, name="mi")
+        for c in range(NCH):
+            nc.scalar.activation(mi[:, c : c + 1], turned[:, c, MEAN_ROW : MEAN_ROW + 1], IDENT, bias=zero[:], scale=inv_c[:, c : c + 1])
 
         pairs = [keep.tile([P, 2 * T], BF16, name="pair%d" % u, tag="pair%d" % u) for u in range(2)]
 
@@ -116,10 +115,11 @@ def tile_picked_lnfold_none_l_kernel(tc, xT, mean, inv, gsum, b, w1_words, w1_sc
             if LOADS[i][0] == 1:
                 cast(i)
         gm_ps = psum.tile([P, S], F32, name="gm_ps")
-        gm_t = [keep.tile([P, N], F32, name="gm_t%d" % c) for c in range(NCH)]
+        gm_all = keep.tile([P, NCH * N], F32, name="gm_all", tag="raw2")
+        gm_t = [gm_all[:, c * N : (c + 1) * N] for c in range(NCH)]
         for c in range(NCH):
-            nc.scalar.activation(gm_t[c][:], g_ps[:], COPY, scale=mi[:, c : c + 1])
-            nc.tensor.transpose(gm_ps[:, c * CH : (c + 1) * CH], gm_t[c][:], ident[:])
+            nc.scalar.activation(gm_t[c], g_ps[:], COPY, scale=mi[:, c : c + 1])
+            nc.tensor.transpose(gm_ps[:, c * CH : (c + 1) * CH], gm_t[c], ident[:])
         nc.scalar.copy(inv_bc[:], inv_ps[:])
 
         codes = [keep.tile([P, CH], U32, name="codes%d" % c, align_bytes=64) for c in range(NCH)]

@@ -25,7 +25,7 @@ P = 128
 CH = 128
 NCH = S // CH
 MEAN_ROW, INV_ROW = P - 2, P - 1
-LOADS = [(0, 0, 512, [("s", 0, 512)]), (0, 512, 1024, [("v", 512, 896), ("s", 896, 1024)]), (1, 0, 512, [("s", 0, 512)]), (1, 512, 896, [("v", 512, 896)]), (1, 896, 1024, [("v", 896, 1024)])]
+LOADS = [(0, 0, 384, [("s", 0, 384)]), (0, 384, 1024, [("v", 384, 832), ("s", 832, 1024)]), (1, 0, 512, [("s", 0, 512)]), (1, 512, 896, [("v", 512, 896)]), (1, 896, 1024, [("v", 896, 1024)])]
 STEPPED = ()
 
 
@@ -42,7 +42,7 @@ def tile_picked_lnfold_none_l_kernel(tc, xT, mean, inv, gsum, b, w1_words, w1_sc
         g_col = keep.tile([P, 1], F32, name="g_col")
         nc.sync.dma_start(stats[MEAN_ROW : MEAN_ROW + 1, :], mean[0:1, :])
         nc.sync.dma_start(stats[INV_ROW : INV_ROW + 1, :], inv[0:1, :])
-        nc.scalar.dma_start(g_col[:], gsum)
+        nc.sync.dma_start(g_col[:], gsum)
         zero = keep.tile([P, 1], F32, name="zero", tag="pair1")
         warm = keep.tile([P, 1], F32, name="warm")
         nc.vector.memset(zero[:], 0.0)
@@ -53,7 +53,7 @@ def tile_picked_lnfold_none_l_kernel(tc, xT, mean, inv, gsum, b, w1_words, w1_sc
         raws = []
         for i, (u, c0, c1, shares) in enumerate(LOADS):
             raw = keep.tile([P, 2, c1 - c0], F32, name="raw%d" % i, tag="raw%d" % i)
-            nc.sync.dma_start(raw[:], x_rows[:, 2 * u : 2 * u + 2, c0:c1])
+            (nc.scalar if i == 0 else nc.sync).dma_start(raw[:], x_rows[:, 2 * u : 2 * u + 2, c0:c1])
             raws.append(raw)
 
         b_col = keep.tile([P, 1], F32, name="b_col")

@@ -4,8 +4,9 @@ import concourse.mybir as mybir
 from concourse.masks import make_identity
 
 K, T, S, N = 512, 1024, 512, 128
+P = 128
 FLOPS = 2 * K * N * S
-BYTES = K * T * 4 + 2 * T * 4 + 2 * N * 4 + 128 * 256 + 16 * 128 + 128 * 32 * 2 + N * S * 4
+BYTES = 4 * K * T + 2 * 4 * T + 2 * 4 * N + P * 2 * N + 16 * N + P * (S // 16) * 2 + 4 * N * S
 
 F32 = mybir.dt.float32
 BF16 = mybir.dt.bfloat16
@@ -18,15 +19,26 @@ FP4X4 = mybir.dt.float4_e2m1fn_x4
 MULT = mybir.AluOpType.mult
 ADD = mybir.AluOpType.add
 SUB = mybir.AluOpType.subtract
-IDENT = mybir.ActivationFunctionType.Identity
 COPY = mybir.ActivationFunctionType.Copy
+IDENT = mybir.ActivationFunctionType.Identity
 
-P = 128
-CH = 128
-NCH = S // CH
+CHUNK = 128
+CHUNKS = S // CHUNK
+LIST_COLS = CHUNK // 16
 MEAN_ROW, INV_ROW = P - 2, P - 1
-LOADS = [(0, 0, 384, [("s", 0, 384)]), (0, 384, 1024, [("v", 384, 832), ("s", 832, 1024)]), (1, 0, 512, [("s", 0, 512)]), (1, 512, 896, [("v", 512, 896)]), (1, 896, 1024, [("v", 896, 1024)])]
-STEPPED = ()
+
+FIRST_PIECE = 384
+VECTOR_SHARE_END = 832
+HALF = T // 2
+LAST_PIECE = T - 128
+PIECES = [
+    (0, 0, FIRST_PIECE, [("scalar", 0, FIRST_PIECE)]),
+    (0, FIRST_PIECE, T, [("vector", FIRST_PIECE, VECTOR_SHARE_END), ("scalar", VECTOR_SHARE_END, T)]),
+    (1, 0, HALF, [("scalar", 0, HALF)]),
+    (1, HALF, LAST_PIECE, [("vector", HALF, LAST_PIECE)]),
+    (1, LAST_PIECE, T, [("vector", LAST_PIECE, T)]),
+]
+SCALAR_PAIR1_PIECE = 2
 
 
 def tile_picked_lnfold_none_l_kernel(tc, xT, mean, inv, gsum, b, w1_words, w1_scales, offs, out):
@@ -34,6 +46,9 @@ def tile_picked_lnfold_none_l_kernel(tc, xT, mean, inv, gsum, b, w1_words, w1_sc
     with ExitStack() as ctx:
         keep = ctx.enter_context(tc.tile_pool(name="keep", bufs=1))
         psum = ctx.enter_context(tc.psum_pool(name="psum", bufs=1))
+
+        def chunk_cols(c):
+            return slice(c * CHUNK, (c + 1) * CHUNK)
 
         offsets = keep.tile([P, S // 16], U16, name="offsets")
         nc.sync.dma_start(offsets[:], offs)
@@ -44,23 +59,23 @@ def tile_picked_lnfold_none_l_kernel(tc, xT, mean, inv, gsum, b, w1_words, w1_sc
         nc.sync.dma_start(stats[INV_ROW : INV_ROW + 1, :], inv[0:1, :])
         nc.sync.dma_start(g_col[:], gsum)
         zero = keep.tile([P, 1], F32, name="zero", tag="pair1")
-        warm = keep.tile([P, 1], F32, name="warm")
-        nc.vector.memset(zero[:], 0.0)
-        nc.scalar.activation(warm[:], zero[:], IDENT, bias=zero[:])
+        cleared = keep.tile([P, 1], F32, name="cleared")
+        nc.vector.memset(cleared[:], 0.0)
+        nc.scalar.activation(zero[:], cleared[:], COPY)
         nc.vector.memset(stats[0:MEAN_ROW, :], 0.0)
 
-        x_rows = xT.rearrange("(p j) w -> p j w", j=4)
+        x_rows = xT.rearrange("(p t) w -> p t w", t=4)
         raws = []
-        for i, (u, c0, c1, shares) in enumerate(LOADS):
-            raw = keep.tile([P, 2, c1 - c0], F32, name="raw%d" % i, tag="raw%d" % i)
-            (nc.scalar if i == 0 else nc.sync).dma_start(raw[:], x_rows[:, 2 * u : 2 * u + 2, c0:c1])
+        for i, (u, first, end, shares) in enumerate(PIECES):
+            raw = keep.tile([P, 2, end - first], F32, name="raw%d" % i, tag="raw%d" % i)
+            queue = nc.scalar if i == 0 else nc.sync
+            queue.dma_start(raw[:], x_rows[:, 2 * u : 2 * u + 2, first:end])
             raws.append(raw)
 
         b_col = keep.tile([P, 1], F32, name="b_col")
         w_words = keep.tile([P, 2 * N], U8, name="w_words", align_bytes=64)
         w_scales = keep.tile([P, N], U8, name="w_scales", align_bytes=64)
         nc.sync.dma_start(w_words[:].bitcast(I32), w1_words[0].bitcast(I32))
-
         ident = keep.tile([P, P], F32, name="ident")
         make_identity(nc, ident[:])
         nc.gpsimd.memset(w_scales[:].bitcast(I32), 0)
@@ -69,76 +84,85 @@ def tile_picked_lnfold_none_l_kernel(tc, xT, mean, inv, gsum, b, w1_words, w1_sc
         nc.sync.dma_start(b_col[:], b)
 
         picked = [keep.tile([P, S // 2], F32, name="picked%d" % h) for h in range(2)]
-        turned = psum.tile([P, NCH, P], F32, name="turned")
+        turned = psum.tile([P, CHUNKS, P], F32, name="turned")
         for h in range(2):
-            nc.vector.tensor_copy(picked[h][:], stats[:].indirect(offsets[:, 16 * h : 16 * (h + 1)]))
+            nc.vector.tensor_copy(picked[h][:], stats[:].indirect(offsets[:, 2 * LIST_COLS * h : 2 * LIST_COLS * (h + 1)]))
             for c in range(2):
-                nc.tensor.transpose(turned[:, 2 * h + c, :], picked[h][:, c * CH : (c + 1) * CH], ident[:])
-        g_ps = psum.tile([P, N], F32, name="g_ps")
-        nc.tensor.transpose(g_ps[:], g_col[:].to_broadcast([P, P]), ident[:])
-        inv_c = keep.tile([P, NCH], F32, name="inv_c")
-        nc.scalar.copy(inv_c[:], turned[:, :, INV_ROW])
-        inv_ps = psum.tile([P, S], F32, name="inv_ps")
-        for c in range(NCH):
-            nc.tensor.transpose(inv_ps[:, c * CH : (c + 1) * CH], inv_c[:, c : c + 1].to_broadcast([P, P]), ident[:])
-        mi = keep.tile([P, NCH], F32, name="mi")
-        for c in range(NCH):
-            nc.scalar.activation(mi[:, c : c + 1], turned[:, c, MEAN_ROW : MEAN_ROW + 1], IDENT, bias=zero[:], scale=inv_c[:, c : c + 1])
+                nc.tensor.transpose(turned[:, 2 * h + c, :], picked[h][:, chunk_cols(c)], ident[:])
+
+        g_rows = psum.tile([P, N], F32, name="g_rows")
+        nc.tensor.transpose(g_rows[:], g_col[:].to_broadcast([P, P]), ident[:])
+        inv_cols = keep.tile([P, CHUNKS], F32, name="inv_cols")
+        nc.scalar.copy(inv_cols[:], turned[:, :, INV_ROW])
+        inv_rows = psum.tile([P, S], F32, name="inv_rows")
+        for c in range(CHUNKS):
+            nc.tensor.transpose(inv_rows[:, chunk_cols(c)], inv_cols[:, c : c + 1].to_broadcast([P, P]), ident[:])
+        mean_inv = keep.tile([P, CHUNKS], F32, name="mean_inv")
+        for c in range(CHUNKS):
+            nc.scalar.activation(mean_inv[:, c : c + 1], turned[:, c, MEAN_ROW : MEAN_ROW + 1], IDENT, bias=zero[:], scale=inv_cols[:, c : c + 1])
 
         pairs = [keep.tile([P, 2 * T], BF16, name="pair%d" % u, tag="pair%d" % u) for u in range(2)]
+        gathered = [keep.tile([P, 2, CHUNK], U32, name="gathered%d" % c) for c in range(CHUNKS)]
+        woven = [keep.tile([P, CHUNK, 2], U32, name="woven%d" % c, tag="woven%d" % c, align_bytes=64) for c in range(CHUNKS)]
+        inv_sb = keep.tile([P, S], F32, name="inv_sb")
 
-        def cast(i):
-            u, c0, c1, shares = LOADS[i]
-            for eng, a, z in shares:
-                dst = pairs[u][:, 2 * a : 2 * z].rearrange("p (c j) -> p c j", j=2)
-                src = raws[i][:, :, a - c0 : z - c0].rearrange("p j c -> p c j")
-                if eng == "v":
-                    nc.vector.tensor_copy(dst, src)
-                else:
-                    nc.scalar.copy(dst, src)
+        def round_pair(pair):
+            for raw, (u, first, end, shares) in zip(raws, PIECES):
+                if u != pair:
+                    continue
+                for engine, lo, hi in shares:
+                    dst = pairs[u][:, 2 * lo : 2 * hi].rearrange("p (w t) -> p w t", t=2)
+                    src = raw[:, :, lo - first : hi - first].rearrange("p t w -> p w t")
+                    if engine == "vector":
+                        nc.vector.tensor_copy(dst, src)
+                    else:
+                        nc.scalar.copy(dst, src)
 
-        halves = [keep.tile([P, 2, CH], U32, name="halves%d" % c, tag="halves%d" % c) for c in range(NCH)]
-        woven = [keep.tile([P, CH, 2], U32, name="woven%d" % c, tag="woven%d" % c, align_bytes=64) for c in range(NCH)]
+        def gather_pair(u, c):
+            window = pairs[u][:].bitcast(U32)
+            nc.vector.tensor_copy(gathered[c][:, u, :], window.indirect(offsets[:, c * LIST_COLS : (c + 1) * LIST_COLS]))
 
-        def gather(u, c):
-            dst = woven[c][:, :, u] if c in STEPPED else halves[c][:, u, :]
-            nc.vector.tensor_copy(dst, pairs[u][:].bitcast(U32).indirect(offsets[:, c * (CH // 16) : (c + 1) * (CH // 16)]))
+        round_pair(0)
+        for c in range(CHUNKS):
+            gather_pair(0, c)
+        round_pair(1)
 
-        inv_bc = keep.tile([P, S], F32, name="inv_bc")
+        shift = psum.tile([P, S], F32, name="shift")
+        shift_t = keep.tile([P, CHUNKS * N], F32, name="shift_t", tag="raw%d" % SCALAR_PAIR1_PIECE)
+        for c in range(CHUNKS):
+            nc.scalar.activation(shift_t[:, c * N : (c + 1) * N], g_rows[:], COPY, scale=mean_inv[:, c : c + 1])
+            nc.tensor.transpose(shift[:, chunk_cols(c)], shift_t[:, c * N : (c + 1) * N], ident[:])
+        nc.scalar.copy(inv_sb[:], inv_rows[:])
 
-        for i in range(len(LOADS)):
-            if LOADS[i][0] == 0:
-                cast(i)
-        for c in range(NCH):
-            gather(0, c)
-        for i in range(len(LOADS)):
-            if LOADS[i][0] == 1:
-                cast(i)
-        gm_ps = psum.tile([P, S], F32, name="gm_ps")
-        gm_all = keep.tile([P, NCH * N], F32, name="gm_all", tag="raw2")
-        gm_t = [gm_all[:, c * N : (c + 1) * N] for c in range(NCH)]
-        for c in range(NCH):
-            nc.scalar.activation(gm_t[c], g_ps[:], COPY, scale=mi[:, c : c + 1])
-            nc.tensor.transpose(gm_ps[:, c * CH : (c + 1) * CH], gm_t[c], ident[:])
-        nc.scalar.copy(inv_bc[:], inv_ps[:])
+        codes = [keep.tile([P, CHUNK], U32, name="codes%d" % c, align_bytes=64) for c in range(CHUNKS)]
+        scales = [keep.tile([P, CHUNK], U8, name="scales%d" % c, align_bytes=64) for c in range(CHUNKS)]
+        ys = [psum.tile([P, CHUNK], F32, name="y%d" % c) for c in range(CHUNKS)]
+        results = [keep.tile([P, CHUNK], F32, name="result%d" % c) for c in range(CHUNKS)]
 
-        codes = [keep.tile([P, CH], U32, name="codes%d" % c, align_bytes=64) for c in range(NCH)]
-        planes = [keep.tile([P, CH], U8, name="plane%d" % c, align_bytes=64) for c in range(NCH)]
-        accs = [psum.tile([P, CH], F32, name="acc%d" % c) for c in range(NCH)]
-        scaled = [keep.tile([P, CH], F32, name="scaled%d" % c) for c in range(NCH)]
-        result = [keep.tile([P, CH], F32, name="result%d" % c) for c in range(NCH)]
+        for c in range(CHUNKS):
+            gather_pair(1, c)
+            nc.scalar.copy(woven[c][:], gathered[c][:].rearrange("p u j -> p j u"))
+        for c in range(CHUNKS):
+            nc.vector.quantize_mx(
+                out=codes[c][:].bitcast(FP8X4),
+                scales=scales[c][:],
+                in_=woven[c][:].rearrange("p j u -> p (j u)").bitcast(BF16),
+            )
+            nc.tensor.matmul_mx(
+                ys[c][:],
+                lhsT=w_words[:].bitcast(FP4X4),
+                lhsT_scale=w_scales[:],
+                rhs=codes[c][:].bitcast(FP8X4),
+                rhs_scale=scales[c][:],
+                start=True,
+                stop=True,
+            )
 
-        for c in range(NCH):
-            gather(1, c)
-            if c not in STEPPED:
-                nc.scalar.copy(woven[c][:], halves[c][:].rearrange("p u s -> p s u"))
-        for c in range(NCH):
-            nc.vector.quantize_mx(out=codes[c][:].bitcast(FP8X4), scales=planes[c][:], in_=woven[c][:].rearrange("p s u -> p (s u)").bitcast(BF16))
-            nc.tensor.matmul_mx(accs[c][:], lhsT=w_words[:].bitcast(FP4X4), lhsT_scale=w_scales[:], rhs=codes[c][:].bitcast(FP8X4), rhs_scale=planes[c][:], start=True, stop=True)
-        for kind, c in [("m", 0), ("m", 1), ("a", 0), ("m", 2), ("a", 1), ("m", 3), ("a", 2), ("a", 3)]:
-            cs = slice(c * CH, (c + 1) * CH)
-            if kind == "m":
-                nc.vector.tensor_tensor(scaled[c][:], accs[c][:], inv_bc[:, cs], MULT)
-            else:
-                nc.vector.scalar_tensor_tensor(result[c][:], scaled[c][:], b_col[:], gm_ps[:, cs], ADD, SUB)
-                nc.sync.dma_start(out[:, cs], result[c][:])
+        scaled = keep.tile([P, S], F32, name="scaled", tag="woven%d" % (CHUNKS - 1), align_bytes=64)
+        for step in range(CHUNKS + 1):
+            if step < CHUNKS:
+                nc.vector.tensor_tensor(scaled[:, chunk_cols(step)], ys[step][:], inv_sb[:, chunk_cols(step)], MULT)
+            if step > 0:
+                cols = chunk_cols(step - 1)
+                nc.vector.scalar_tensor_tensor(results[step - 1][:], scaled[:, cols], b_col[:], shift[:, cols], ADD, SUB)
+                nc.sync.dma_start(out[:, cols], results[step - 1][:])

from contextlib import ExitStack

import concourse.mybir as mybir
from concourse.masks import make_identity

K, T, S, N = 512, 1024, 512, 128
P = 128
FLOPS = 2 * K * N * S
BYTES = 4 * K * T + 2 * 4 * T + 2 * 4 * N + P * 2 * N + 16 * N + P * (S // 16) * 2 + 4 * N * S

F32 = mybir.dt.float32
BF16 = mybir.dt.bfloat16
U32 = mybir.dt.uint32
I32 = mybir.dt.int32
U16 = mybir.dt.uint16
U8 = mybir.dt.uint8
FP8X4 = mybir.dt.float8_e4m3fn_x4
FP4X4 = mybir.dt.float4_e2m1fn_x4
MULT = mybir.AluOpType.mult
ADD = mybir.AluOpType.add
SUB = mybir.AluOpType.subtract
COPY = mybir.ActivationFunctionType.Copy
IDENT = mybir.ActivationFunctionType.Identity

CHUNK = 128
CHUNKS = S // CHUNK
LIST_COLS = CHUNK // 16
MEAN_ROW, INV_ROW = P - 2, P - 1

FIRST_PIECE = 384
VECTOR_SHARE_END = 832
HALF = T // 2
LAST_PIECE = T - 128
PIECES = [
    (0, 0, FIRST_PIECE, [("scalar", 0, FIRST_PIECE)]),
    (0, FIRST_PIECE, T, [("vector", FIRST_PIECE, VECTOR_SHARE_END), ("scalar", VECTOR_SHARE_END, T)]),
    (1, 0, HALF, [("scalar", 0, HALF)]),
    (1, HALF, LAST_PIECE, [("vector", HALF, LAST_PIECE)]),
    (1, LAST_PIECE, T, [("vector", LAST_PIECE, T)]),
]
SCALAR_PAIR1_PIECE = 2


def tile_picked_lnfold_none_l_kernel(tc, xT, mean, inv, gsum, b, w1_words, w1_scales, offs, out):
    nc = tc.nc
    with ExitStack() as ctx:
        keep = ctx.enter_context(tc.tile_pool(name="keep", bufs=1))
        psum = ctx.enter_context(tc.psum_pool(name="psum", bufs=1))

        def chunk_cols(c):
            return slice(c * CHUNK, (c + 1) * CHUNK)

        offsets = keep.tile([P, S // 16], U16, name="offsets")
        nc.sync.dma_start(offsets[:], offs)

        stats = keep.tile([P, T], F32, name="stats")
        g_col = keep.tile([P, 1], F32, name="g_col")
        nc.sync.dma_start(stats[MEAN_ROW : MEAN_ROW + 1, :], mean[0:1, :])
        nc.sync.dma_start(stats[INV_ROW : INV_ROW + 1, :], inv[0:1, :])
        nc.sync.dma_start(g_col[:], gsum)
        zero = keep.tile([P, 1], F32, name="zero", tag="pair1")
        cleared = keep.tile([P, 1], F32, name="cleared")
        nc.vector.memset(cleared[:], 0.0)
        nc.scalar.activation(zero[:], cleared[:], COPY)
        nc.vector.memset(stats[0:MEAN_ROW, :], 0.0)

        x_rows = xT.rearrange("(p t) w -> p t w", t=4)
        raws = []
        for i, (u, first, end, shares) in enumerate(PIECES):
            raw = keep.tile([P, 2, end - first], F32, name="raw%d" % i, tag="raw%d" % i)
            queue = nc.scalar if i == 0 else nc.sync
            queue.dma_start(raw[:], x_rows[:, 2 * u : 2 * u + 2, first:end])
            raws.append(raw)

        b_col = keep.tile([P, 1], F32, name="b_col")
        w_words = keep.tile([P, 2 * N], U8, name="w_words", align_bytes=64)
        w_scales = keep.tile([P, N], U8, name="w_scales", align_bytes=64)
        nc.sync.dma_start(w_words[:].bitcast(I32), w1_words[0].bitcast(I32))
        ident = keep.tile([P, P], F32, name="ident")
        make_identity(nc, ident[:])
        nc.gpsimd.memset(w_scales[:].bitcast(I32), 0)
        for q in range(4):
            nc.sync.dma_start(w_scales[32 * q : 32 * q + 4, :].bitcast(I32), w1_scales[0, 4 * q : 4 * q + 4, :].bitcast(I32))
        nc.sync.dma_start(b_col[:], b)

        picked = [keep.tile([P, S // 2], F32, name="picked%d" % h) for h in range(2)]
        turned = psum.tile([P, CHUNKS, P], F32, name="turned")
        for h in range(2):
            nc.vector.tensor_copy(picked[h][:], stats[:].indirect(offsets[:, 2 * LIST_COLS * h : 2 * LIST_COLS * (h + 1)]))
            for c in range(2):
                nc.tensor.transpose(turned[:, 2 * h + c, :], picked[h][:, chunk_cols(c)], ident[:])

        g_rows = psum.tile([P, N], F32, name="g_rows")
        nc.tensor.transpose(g_rows[:], g_col[:].to_broadcast([P, P]), ident[:])
        inv_cols = keep.tile([P, CHUNKS], F32, name="inv_cols")
        nc.scalar.copy(inv_cols[:], turned[:, :, INV_ROW])
        inv_rows = psum.tile([P, S], F32, name="inv_rows")
        for c in range(CHUNKS):
            nc.tensor.transpose(inv_rows[:, chunk_cols(c)], inv_cols[:, c : c + 1].to_broadcast([P, P]), ident[:])
        mean_inv = keep.tile([P, CHUNKS], F32, name="mean_inv")
        for c in range(CHUNKS):
            nc.scalar.activation(mean_inv[:, c : c + 1], turned[:, c, MEAN_ROW : MEAN_ROW + 1], IDENT, bias=zero[:], scale=inv_cols[:, c : c + 1])

        pairs = [keep.tile([P, 2 * T], BF16, name="pair%d" % u, tag="pair%d" % u) for u in range(2)]
        gathered = [keep.tile([P, 2, CHUNK], U32, name="gathered%d" % c) for c in range(CHUNKS)]
        woven = [keep.tile([P, CHUNK, 2], U32, name="woven%d" % c, tag="woven%d" % c, align_bytes=64) for c in range(CHUNKS)]
        inv_sb = keep.tile([P, S], F32, name="inv_sb")

        def round_pair(pair):
            for raw, (u, first, end, shares) in zip(raws, PIECES):
                if u != pair:
                    continue
                for engine, lo, hi in shares:
                    dst = pairs[u][:, 2 * lo : 2 * hi].rearrange("p (w t) -> p w t", t=2)
                    src = raw[:, :, lo - first : hi - first].rearrange("p t w -> p w t")
                    if engine == "vector":
                        nc.vector.tensor_copy(dst, src)
                    else:
                        nc.scalar.copy(dst, src)

        def gather_pair(u, c):
            window = pairs[u][:].bitcast(U32)
            nc.vector.tensor_copy(gathered[c][:, u, :], window.indirect(offsets[:, c * LIST_COLS : (c + 1) * LIST_COLS]))

        round_pair(0)
        for c in range(CHUNKS):
            gather_pair(0, c)
        round_pair(1)

        shift = psum.tile([P, S], F32, name="shift")
        shift_t = keep.tile([P, CHUNKS * N], F32, name="shift_t", tag="raw%d" % SCALAR_PAIR1_PIECE)
        for c in range(CHUNKS):
            nc.scalar.activation(shift_t[:, c * N : (c + 1) * N], g_rows[:], COPY, scale=mean_inv[:, c : c + 1])
            nc.tensor.transpose(shift[:, chunk_cols(c)], shift_t[:, c * N : (c + 1) * N], ident[:])
        nc.scalar.copy(inv_sb[:], inv_rows[:])

        codes = [keep.tile([P, CHUNK], U32, name="codes%d" % c, align_bytes=64) for c in range(CHUNKS)]
        scales = [keep.tile([P, CHUNK], U8, name="scales%d" % c, align_bytes=64) for c in range(CHUNKS)]
        ys = [psum.tile([P, CHUNK], F32, name="y%d" % c) for c in range(CHUNKS)]
        results = [keep.tile([P, CHUNK], F32, name="result%d" % c) for c in range(CHUNKS)]

        for c in range(CHUNKS):
            gather_pair(1, c)
            nc.scalar.copy(woven[c][:], gathered[c][:].rearrange("p u j -> p j u"))
        for c in range(CHUNKS):
            nc.vector.quantize_mx(
                out=codes[c][:].bitcast(FP8X4),
                scales=scales[c][:],
                in_=woven[c][:].rearrange("p j u -> p (j u)").bitcast(BF16),
            )
            nc.tensor.matmul_mx(
                ys[c][:],
                lhsT=w_words[:].bitcast(FP4X4),
                lhsT_scale=w_scales[:],
                rhs=codes[c][:].bitcast(FP8X4),
                rhs_scale=scales[c][:],
                start=True,
                stop=True,
            )

        scaled = keep.tile([P, S], F32, name="scaled", tag="woven%d" % (CHUNKS - 1), align_bytes=64)
        for step in range(CHUNKS + 1):
            if step < CHUNKS:
                nc.vector.tensor_tensor(scaled[:, chunk_cols(step)], ys[step][:], inv_sb[:, chunk_cols(step)], MULT)
            if step > 0:
                cols = chunk_cols(step - 1)
                nc.vector.scalar_tensor_tensor(results[step - 1][:], scaled[:, cols], b_col[:], shift[:, cols], ADD, SUB)
                nc.sync.dma_start(out[:, cols], results[step - 1][:])
